import numpy as np
import ml_dtypes


def mxq(x, axis, fmt="e4m3"):
    dtype, down = {"e4m3": (ml_dtypes.float8_e4m3fn, 7), "e5m2": (ml_dtypes.float8_e5m2, 14)}[fmt]
    v = np.moveaxis(np.asarray(x, np.float32).astype(ml_dtypes.bfloat16).astype(np.float64), axis, -1)
    blocks = v.reshape(v.shape[:-1] + (-1, 32))
    amax = np.abs(blocks).max(-1, keepdims=True)
    byte = np.maximum(np.where(amax > 0, np.frexp(amax)[1] - 1 + 127, 0) - down, 1)
    scale = np.exp2(byte - 127.0)
    codes = (blocks / scale).astype(np.float32).astype(dtype).astype(np.float64)
    return np.moveaxis((codes * scale).reshape(v.shape), -1, axis)


WIDE = False


def mx_kscale(k):
    if not WIDE:
        return np.ones(k)
    levels = np.array([10, -10, 5, -5, 0])
    if k % 512:
        return np.exp2(np.random.permutation(np.resize(levels, k // 32))).repeat(32)
    a = np.empty((k // 512, 16))
    for p in range(k // 512):
        a[p, :8] = np.random.permutation(np.resize(levels, 8))
        for g in range(8):
            far = levels[np.abs(levels - a[p, g]) >= 10]
            a[p, g + 8] = far[np.random.randint(len(far))]
    return np.exp2(a.ravel()).repeat(32)


def f64(x):
    return np.asarray(x).astype(np.float64)


def striped(idx):
    return np.tile(np.asarray(idx).reshape(-1, 16).T, (8, 1)).astype(np.uint16)


def unstriped(offs):
    return offs[:16].T.reshape(-1).astype(np.int64)


E2M1 = np.array([0.0, 0.5, 1.0, 1.5, 2.0, 3.0, 4.0, 6.0, -0.0, -0.5, -1.0, -1.5, -2.0, -3.0, -4.0, -6.0])


def pack_weight(w, fmt):
    k, n = w.shape
    w = f64(np.asarray(w, np.float32).astype(ml_dtypes.bfloat16)).reshape(k // 32, 32, n)
    amax = np.abs(w).max(1)
    if fmt == "e4m3":
        byte = np.frexp(amax)[1] - 1 + 127 - 7
    else:
        mant, ex = np.frexp(amax / 6.0)
        byte = np.where(mant > 0.5, ex, ex - 1) + 127
    byte = np.clip(np.where(amax > 0, byte, 1), 1, 254)
    scaled = (w * np.exp2(127.0 - byte)[:, None, :]).reshape(k, n).astype(np.float32)
    by_word = np.ascontiguousarray(scaled.reshape(k // 512, 128, 4, n).transpose(0, 1, 3, 2))
    if fmt == "e4m3":
        words = by_word.astype(ml_dtypes.float8_e4m3fn).view(np.uint8)
    else:
        c = by_word.astype(ml_dtypes.float4_e2m1fn).view(np.uint8) & 0xF
        words = (c[..., 0::2] | (c[..., 1::2] << 4)).reshape(k // 512, 128, 2 * n)
    return np.ascontiguousarray(words), np.ascontiguousarray(byte.astype(np.uint8).reshape(k // 512, 16, n))


def unpack_weight(words, scales, fmt):
    g, _, n = scales.shape
    words = np.ascontiguousarray(words).reshape(g, 128, n, -1)
    if fmt == "e4m3":
        vals = words.view(ml_dtypes.float8_e4m3fn).astype(np.float64)
    else:
        nib = np.empty((g, 128, n, 4), np.uint8)
        nib[..., 0::2] = words & 0xF
        nib[..., 1::2] = words >> 4
        vals = E2M1[nib]
    vals = vals * np.repeat(np.exp2(scales.astype(np.float64) - 127.0), 8, axis=1)[..., None]
    return vals.transpose(0, 1, 3, 2).reshape(g * 512, n)


K, L, T, C, J = 512, 1024, 256, 1024, 512


def setup_inputs():
    n = np.random.standard_normal
    idx = np.random.permutation(C)[:J]
    fk = mx_kscale(K)
    fl = mx_kscale(L)
    wcp = pack_weight(n((K, J)) * 1 / np.sqrt(K) * fk[:, None], "e2m1")
    xlp = pack_weight(n((L, T)) * 0.5 / fl[:, None], "e4m3")
    wlp = pack_weight(n((L, C)) * 1 / np.sqrt(L) * fl[:, None], "e2m1")
    return {
        "xt": (n((K, T)) * 0.5 / fk[:, None]).astype(np.float32),
        "wc_words": wcp[0],
        "wc_scales": wcp[1],
        "xl_words": xlp[0],
        "xl_scales": xlp[1],
        "wl_words": wlp[0],
        "wl_scales": wlp[1],
        "offs": striped(idx),
    }


def reference(xt, wc_words, wc_scales, xl_words, xl_scales, wl_words, wl_scales, offs):
    idx = unstriped(offs)
    wcu = unpack_weight(wc_words, wc_scales, "e2m1")
    xlu = unpack_weight(xl_words, xl_scales, "e4m3")
    wlu = unpack_weight(wl_words, wl_scales, "e2m1")
    xtq = mxq(f64(xt), 0, "e4m3")
    z = xtq.T @ wcu
    u = xlu.T @ wlu
    p = np.exp(z)
    q = np.exp(u[:, idx])
    y = 256.0 * p / np.sum(p, axis=1, keepdims=True) - 256.0 * q / np.sum(q, axis=1, keepdims=True)
    return y

@@ -1,0 +1,165 @@
+from contextlib import ExitStack
+
+import concourse.mybir as mybir
+
+K, L, T, C, J = 512, 1024, 256, 1024, 512
+FLOPS = 2 * T * (K * J + L * C)
+
+F32 = mybir.dt.float32
+BF16 = mybir.dt.bfloat16
+I32 = mybir.dt.int32
+U32 = mybir.dt.uint32
+U16 = mybir.dt.uint16
+U8 = mybir.dt.uint8
+FP8X4 = mybir.dt.float8_e4m3fn_x4
+FP4X4 = mybir.dt.float4_e2m1fn_x4
+ALU = mybir.AluOpType
+ACT = mybir.ActivationFunctionType
+AX = mybir.AxisListType
+
+P = 128
+PACK = 4
+BANK = 512
+QUADS = 4
+PASSES = L // (P * PACK)
+TILES = T // P
+
+
+def load_scales(queues, plane, scales):
+    for q in range(QUADS):
+        queues[q].dma_start(
+            out=plane[32 * q : 32 * q + 4, :, :].bitcast(I32),
+            in_=scales[:, 4 * q : 4 * q + 4, :].rearrange("z r n -> r z n").bitcast(I32),
+        )
+
+
+def tile_list_teacher_at_listed_classes_kernel(
+    tc, xt, wc_words, wc_scales, xl_words, xl_scales, wl_words, wl_scales, offs, out
+):
+    nc = tc.nc
+    with ExitStack() as ctx:
+        keep = ctx.enter_context(tc.tile_pool(name="keep", bufs=1))
+        psum = ctx.enter_context(tc.psum_pool(name="psum", bufs=1))
+
+        offsets = keep.tile([P, J // 16], U16, name="offsets")
+        xt_raw = keep.tile([P, PACK, T], F32, name="xt_raw")
+        wc_codes = keep.tile([P, 2 * J], U8, name="wc_codes", align_bytes=64)
+        wc_plane = keep.tile([P, 1, J], U8, name="wc_plane", align_bytes=64)
+        xl_codes = keep.tile([P, PASSES, T], U32, name="xl_codes", align_bytes=64)
+        xl_plane = keep.tile([P, PASSES, T], U8, name="xl_plane", align_bytes=64)
+        wl_codes = keep.tile([P, PASSES, 2 * C], U8, name="wl_codes", align_bytes=64)
+        wl_plane = keep.tile([P, PASSES, C], U8, name="wl_plane", align_bytes=64)
+
+        for plane in (wc_plane, wl_plane, xl_plane):
+            nc.vector.memset(plane[:].bitcast(I32), 0)
+
+        nc.sync.dma_start(offsets[:], offs)
+        nc.sync.dma_start(out=xt_raw[:], in_=xt.rearrange("(p j) t -> p j t", j=PACK))
+        nc.sync.dma_start(out=wc_codes[:].bitcast(I32), in_=wc_words[0].bitcast(I32))
+        load_scales([nc.scalar] * 4, wc_plane, wc_scales)
+        nc.gpsimd.dma_start(
+            out=wl_codes[:].bitcast(I32),
+            in_=wl_words.rearrange("z p b -> p z b").bitcast(I32),
+        )
+        nc.gpsimd.dma_start(
+            out=xl_codes[:].bitcast(I32),
+            in_=xl_words.rearrange("z p c r -> p z (c r)").bitcast(I32),
+        )
+        load_scales([nc.sync] * 4, wl_plane, wl_scales)
+        load_scales([nc.sync] * 4, xl_plane, xl_scales)
+
+        warm_in = keep.tile([P, 1], F32, name="warm_in")
+        warm_out = keep.tile([P, 1], F32, name="warm_out")
+        nc.vector.memset(warm_in[:], 0.0)
+        nc.scalar.activation(out=warm_out[:], in_=warm_in[:], func=ACT.Exp)
+
+        grouped, x_codes, x_plane, z, p, p_sum, p_negmax, p_share = [], [], [], [], [], [], [], []
+        for h in range(TILES):
+            grouped.append(keep.tile([P, P, PACK], BF16, name=f"grouped{h}", align_bytes=64))
+            x_codes.append(keep.tile([P, P], U32, name=f"x_codes{h}", align_bytes=64))
+            x_plane.append(keep.tile([P, P], U8, name=f"x_plane{h}", align_bytes=64))
+            nc.vector.tensor_copy(
+                out=grouped[h][:],
+                in_=xt_raw[:, :, h * P : (h + 1) * P].rearrange("p j t -> p t j"),
+            )
+        for h in range(TILES):
+            nc.vector.quantize_mx(
+                out=x_codes[h][:].bitcast(FP8X4),
+                scales=x_plane[h][:],
+                in_=grouped[h][:].rearrange("p t j -> p (t j)"),
+            )
+        for h in range(TILES):
+            z.append(psum.tile([P, J], F32, name=f"z{h}"))
+            nc.tensor.matmul_mx(
+                out=z[h][:],
+                lhsT=x_codes[h][:].bitcast(FP8X4),
+                lhsT_scale=x_plane[h][:],
+                rhs=wc_codes[:].bitcast(FP4X4),
+                rhs_scale=wc_plane[:, 0, :],
+                start=True,
+                stop=True,
+            )
+        for h in range(TILES):
+            p_negmax.append(keep.tile([P, 1], F32, name=f"p_negmax{h}"))
+            nc.vector.tensor_reduce(
+                out=p_negmax[h][:], in_=z[h][:], axis=AX.X, op=ALU.max, negate=True
+            )
+
+        u = []
+        for h in range(TILES):
+            u.append(keep.tile([P, C], F32, name=f"u{h}", tag=f"u{h}"))
+            for b in range(C // BANK):
+                acc = psum.tile([P, BANK], F32, name=f"acc{h}{b}")
+                for g in range(PASSES):
+                    nc.tensor.matmul_mx(
+                        out=acc[:],
+                        lhsT=xl_codes[:, g, h * P : (h + 1) * P].bitcast(FP8X4),
+                        lhsT_scale=xl_plane[:, g, h * P : (h + 1) * P],
+                        rhs=wl_codes[:, g, 2 * b * BANK : 2 * (b + 1) * BANK].bitcast(FP4X4),
+                        rhs_scale=wl_plane[:, g, b * BANK : (b + 1) * BANK],
+                        start=(g == 0),
+                        stop=(g == PASSES - 1),
+                    )
+                if h == 0 and b == 1:
+                    nc.vector.tensor_copy(out=u[h][:, b * BANK : (b + 1) * BANK], in_=acc[:])
+                else:
+                    nc.scalar.copy(out=u[h][:, b * BANK : (b + 1) * BANK], in_=acc[:])
+
+        q, q_sum = [], []
+        for h in range(TILES):
+            listed = keep.tile([P, J], F32, name=f"listed{h}")
+            q_negmax = keep.tile([P, 1], F32, name=f"q_negmax{h}")
+            q.append(keep.tile([P, J], F32, name=f"q{h}"))
+            q_sum.append(keep.tile([P, 1], F32, name=f"q_sum{h}"))
+            nc.vector.tensor_copy(listed[:], u[h][:].indirect(offsets[:]))
+            nc.vector.tensor_reduce(
+                out=q_negmax[:], in_=listed[:], axis=AX.X, op=ALU.max, negate=True
+            )
+            nc.scalar.activation(
+                out=q[h][:], in_=listed[:], func=ACT.Exp, bias=q_negmax[:], accum_out=q_sum[h][:]
+            )
+
+        shares = keep.tile([P, C], F32, name="shares", tag="u0")
+        for h in range(TILES):
+            p.append(keep.tile([P, J], F32, name=f"p{h}"))
+            p_sum.append(keep.tile([P, 1], F32, name=f"p_sum{h}"))
+            p_share.append(shares[:, h * J : (h + 1) * J])
+            p_inv = keep.tile([P, 1], F32, name=f"p_inv{h}")
+            p_fac = keep.tile([P, 1], F32, name=f"p_fac{h}")
+            nc.scalar.activation(
+                out=p[h][:], in_=z[h][:], func=ACT.Exp, bias=p_negmax[h][:], accum_out=p_sum[h][:]
+            )
+            nc.vector.reciprocal(out=p_inv[:], in_=p_sum[h][:])
+            nc.vector.tensor_scalar_mul(p_fac[:], p_inv[:], 256.0)
+            nc.scalar.activation(out=p_share[h], in_=p[h][:], func=ACT.Identity, scale=p_fac[:])
+
+        for h in range(TILES):
+            tail = keep.tile([P, C], F32, name=f"tail{h}", tag=("u1" if h == 0 else "tail1"))
+            res, q_inv, q_fac = tail[:, 0:J], tail[:, J : J + 1], tail[:, J + 8 : J + 9]
+            nc.vector.reciprocal(out=q_inv, in_=q_sum[h][:])
+            nc.vector.tensor_scalar_mul(q_fac, q_inv, -256.0)
+            nc.vector.scalar_tensor_tensor(
+                out=res, in0=q[h][:], scalar=q_fac, in1=p_share[h],
+                op0=ALU.mult, op1=ALU.add,
+            )
+            nc.sync.dma_start(out=out[h * P : (h + 1) * P, :], in_=res)

@@ -23,11 +23,19 @@ BANK = 512
 QUADS = 4
 PASSES = L // (P * PACK)
 TILES = T // P
+GAIN = 256.0
 
 
-def load_scales(queues, plane, scales):
+def scale_plane(nc, pool, name, scales):
+    passes, rows, width = scales.shape
+    tile = pool.tile([P, passes * width + 4], U8, name=name, align_bytes=64)
+    nc.vector.memset(tile[:].bitcast(I32), 0)
+    return tile[:, 0 : passes * width].rearrange("p (z n) -> p z n", z=passes)
+
+
+def load_scales(queue, plane, scales):
     for q in range(QUADS):
-        queues[q].dma_start(
+        queue.dma_start(
             out=plane[32 * q : 32 * q + 4, :, :].bitcast(I32),
             in_=scales[:, 4 * q : 4 * q + 4, :].rearrange("z r n -> r z n").bitcast(I32),
         )
@@ -44,19 +52,16 @@ def tile_list_teacher_at_listed_classes_kernel(
         offsets = keep.tile([P, J // 16], U16, name="offsets")
         xt_raw = keep.tile([P, PACK, T], F32, name="xt_raw")
         wc_codes = keep.tile([P, 2 * J], U8, name="wc_codes", align_bytes=64)
-        wc_plane = keep.tile([P, 1, J], U8, name="wc_plane", align_bytes=64)
         xl_codes = keep.tile([P, PASSES, T], U32, name="xl_codes", align_bytes=64)
-        xl_plane = keep.tile([P, PASSES, T], U8, name="xl_plane", align_bytes=64)
         wl_codes = keep.tile([P, PASSES, 2 * C], U8, name="wl_codes", align_bytes=64)
-        wl_plane = keep.tile([P, PASSES, C], U8, name="wl_plane", align_bytes=64)
-
-        for plane in (wc_plane, wl_plane, xl_plane):
-            nc.vector.memset(plane[:].bitcast(I32), 0)
+        wc_plane = scale_plane(nc, keep, "wc_plane", wc_scales)
+        wl_plane = scale_plane(nc, keep, "wl_plane", wl_scales)
+        xl_plane = scale_plane(nc, keep, "xl_plane", xl_scales)
 
         nc.sync.dma_start(offsets[:], offs)
         nc.sync.dma_start(out=xt_raw[:], in_=xt.rearrange("(p j) t -> p j t", j=PACK))
         nc.sync.dma_start(out=wc_codes[:].bitcast(I32), in_=wc_words[0].bitcast(I32))
-        load_scales([nc.scalar] * 4, wc_plane, wc_scales)
+        load_scales(nc.scalar, wc_plane, wc_scales)
         nc.gpsimd.dma_start(
             out=wl_codes[:].bitcast(I32),
             in_=wl_words.rearrange("z p b -> p z b").bitcast(I32),
@@ -65,33 +70,40 @@ def tile_list_teacher_at_listed_classes_kernel(
             out=xl_codes[:].bitcast(I32),
             in_=xl_words.rearrange("z p c r -> p z (c r)").bitcast(I32),
         )
-        load_scales([nc.sync] * 4, wl_plane, wl_scales)
-        load_scales([nc.sync] * 4, xl_plane, xl_scales)
+        load_scales(nc.sync, wl_plane, wl_scales)
+        load_scales(nc.sync, xl_plane, xl_scales)
 
-        warm_in = keep.tile([P, 1], F32, name="warm_in")
-        warm_out = keep.tile([P, 1], F32, name="warm_out")
-        nc.vector.memset(warm_in[:], 0.0)
-        nc.scalar.activation(out=warm_out[:], in_=warm_in[:], func=ACT.Exp)
+        def column(name):
+            return keep.tile([P, 1], F32, name=name)
 
-        grouped, x_codes, x_plane, z, p, p_sum, p_negmax, p_share = [], [], [], [], [], [], [], []
+        def exp_with_sum(name, logits, gain):
+            negmax, total, part = column(name + "_negmax"), column(name + "_sum"), column(name + "_part")
+            e = keep.tile([P, J], F32, name=name)
+            nc.vector.tensor_reduce(out=negmax[:], in_=logits, axis=AX.X, op=ALU.max, negate=True)
+            nc.scalar.activation(out=e[:], in_=logits, func=ACT.Exp, bias=negmax[:], accum_out=total[:])
+            nc.scalar.mul(part[:], total[:], 1.0 / gain)
+            return e, part
+
+        grouped, x_codes, x_plane, z = [], [], [], []
         for h in range(TILES):
             grouped.append(keep.tile([P, P, PACK], BF16, name=f"grouped{h}", align_bytes=64))
-            x_codes.append(keep.tile([P, P], U32, name=f"x_codes{h}", align_bytes=64))
-            x_plane.append(keep.tile([P, P], U8, name=f"x_plane{h}", align_bytes=64))
             nc.vector.tensor_copy(
                 out=grouped[h][:],
                 in_=xt_raw[:, :, h * P : (h + 1) * P].rearrange("p j t -> p t j"),
             )
         for h in range(TILES):
+            x_codes.append(keep.tile([P, P], U32, name=f"x_codes{h}", align_bytes=64))
+            x_plane.append(keep.tile([P, P], U8, name=f"x_plane{h}", align_bytes=64))
             nc.vector.quantize_mx(
                 out=x_codes[h][:].bitcast(FP8X4),
                 scales=x_plane[h][:],
                 in_=grouped[h][:].rearrange("p t j -> p (t j)"),
             )
+        p, p_fac = [], []
         for h in range(TILES):
-            z.append(psum.tile([P, J], F32, name=f"z{h}"))
+            z = psum.tile([P, J], F32, name=f"z{h}")
             nc.tensor.matmul_mx(
-                out=z[h][:],
+                out=z[:],
                 lhsT=x_codes[h][:].bitcast(FP8X4),
                 lhsT_scale=x_plane[h][:],
                 rhs=wc_codes[:].bitcast(FP4X4),
@@ -99,11 +111,10 @@ def tile_list_teacher_at_listed_classes_kernel(
                 start=True,
                 stop=True,
             )
-        for h in range(TILES):
-            p_negmax.append(keep.tile([P, 1], F32, name=f"p_negmax{h}"))
-            nc.vector.tensor_reduce(
-                out=p_negmax[h][:], in_=z[h][:], axis=AX.X, op=ALU.max, negate=True
-            )
+            e, part = exp_with_sum(f"p{h}", z[:], GAIN)
+            p.append(e)
+            p_fac.append(column(f"p_fac{h}"))
+            nc.vector.reciprocal(out=p_fac[h][:], in_=part[:])
 
         u = []
         for h in range(TILES):
@@ -125,41 +136,32 @@ def tile_list_teacher_at_listed_classes_kernel(
                 else:
                     nc.scalar.copy(out=u[h][:, b * BANK : (b + 1) * BANK], in_=acc[:])
 
-        q, q_sum = [], []
-        for h in range(TILES):
+        def gather(h):
             listed = keep.tile([P, J], F32, name=f"listed{h}")
-            q_negmax = keep.tile([P, 1], F32, name=f"q_negmax{h}")
-            q.append(keep.tile([P, J], F32, name=f"q{h}"))
-            q_sum.append(keep.tile([P, 1], F32, name=f"q_sum{h}"))
             nc.vector.tensor_copy(listed[:], u[h][:].indirect(offsets[:]))
-            nc.vector.tensor_reduce(
-                out=q_negmax[:], in_=listed[:], axis=AX.X, op=ALU.max, negate=True
-            )
-            nc.scalar.activation(
-                out=q[h][:], in_=listed[:], func=ACT.Exp, bias=q_negmax[:], accum_out=q_sum[h][:]
-            )
+            return listed
 
-        shares = keep.tile([P, C], F32, name="shares", tag="u0")
-        for h in range(TILES):
-            p.append(keep.tile([P, J], F32, name=f"p{h}"))
-            p_sum.append(keep.tile([P, 1], F32, name=f"p_sum{h}"))
-            p_share.append(shares[:, h * J : (h + 1) * J])
-            p_inv = keep.tile([P, 1], F32, name=f"p_inv{h}")
-            p_fac = keep.tile([P, 1], F32, name=f"p_fac{h}")
-            nc.scalar.activation(
-                out=p[h][:], in_=z[h][:], func=ACT.Exp, bias=p_negmax[h][:], accum_out=p_sum[h][:]
-            )
-            nc.vector.reciprocal(out=p_inv[:], in_=p_sum[h][:])
-            nc.vector.tensor_scalar_mul(p_fac[:], p_inv[:], 256.0)
-            nc.scalar.activation(out=p_share[h], in_=p[h][:], func=ACT.Identity, scale=p_fac[:])
+        def finish(h, q, q_fac, p_share, res, pieces):
+            width = J // len(pieces)
+            for i, queue in enumerate(pieces):
+                cols = slice(i * width, (i + 1) * width)
+                nc.vector.scalar_tensor_tensor(
+                    out=res[:, cols], in0=q[:, cols], scalar=q_fac, in1=p_share[:, cols],
+                    op0=ALU.mult, op1=ALU.add,
+                )
+                queue.dma_start(out=out[h * P : (h + 1) * P, cols], in_=res[:, cols])
 
+        listed0 = gather(0)
+        shares = keep.tile([P, TILES, J], F32, name="shares", tag="u0")
+        q0, q_part0 = exp_with_sum("q0", listed0[:], -GAIN)
         for h in range(TILES):
-            tail = keep.tile([P, C], F32, name=f"tail{h}", tag=("u1" if h == 0 else "tail1"))
-            res, q_inv, q_fac = tail[:, 0:J], tail[:, J : J + 1], tail[:, J + 8 : J + 9]
-            nc.vector.reciprocal(out=q_inv, in_=q_sum[h][:])
-            nc.vector.tensor_scalar_mul(q_fac, q_inv, -256.0)
-            nc.vector.scalar_tensor_tensor(
-                out=res, in0=q[h][:], scalar=q_fac, in1=p_share[h],
-                op0=ALU.mult, op1=ALU.add,
-            )
-            nc.sync.dma_start(out=out[h * P : (h + 1) * P, :], in_=res)
+            nc.scalar.activation(out=shares[:, h, :], in_=p[h][:], func=ACT.Identity, scale=p_fac[h][:])
+        listed1 = gather(1)
+        tail0 = keep.tile([P, J + 1], F32, name="tail0", tag="u1")
+        nc.vector.reciprocal(out=tail0[:, J : J + 1], in_=q_part0[:])
+        q1, q_part1 = exp_with_sum("q1", listed1[:], -GAIN)
+        finish(0, q0, tail0[:, J : J + 1], shares[:, 0, :], tail0, [nc.sync])
+        q_fac1 = column("q_fac1")
+        res1 = keep.tile([P, J], F32, name="res1")
+        nc.vector.reciprocal(out=q_fac1[:], in_=q_part1[:])
+        finish(1, q1, q_fac1[:], shares[:, 1, :], res1, [nc.sync, nc.scalar])

@@ -76,13 +76,12 @@ def tile_list_teacher_at_listed_classes_kernel(
         def column(name):
             return keep.tile([P, 1], F32, name=name)
 
-        def exp_with_sum(name, logits, gain):
-            negmax, total, part = column(name + "_negmax"), column(name + "_sum"), column(name + "_part")
+        def exp_with_sum(name, logits):
+            negmax, total = column(name + "_negmax"), column(name + "_sum")
             e = keep.tile([P, J], F32, name=name)
             nc.vector.tensor_reduce(out=negmax[:], in_=logits, axis=AX.X, op=ALU.max, negate=True)
             nc.scalar.activation(out=e[:], in_=logits, func=ACT.Exp, bias=negmax[:], accum_out=total[:])
-            nc.scalar.mul(part[:], total[:], 1.0 / gain)
-            return e, part
+            return e, total
 
         grouped, x_codes, x_plane, z = [], [], [], []
         for h in range(TILES):
@@ -111,10 +110,23 @@ def tile_list_teacher_at_listed_classes_kernel(
                 start=True,
                 stop=True,
             )
-            e, part = exp_with_sum(f"p{h}", z[:], GAIN)
+            e, total = exp_with_sum(f"p{h}", z[:])
             p.append(e)
+            p_inv = column(f"p_inv{h}")
             p_fac.append(column(f"p_fac{h}"))
-            nc.vector.reciprocal(out=p_fac[h][:], in_=part[:])
+            nc.vector.reciprocal(out=p_inv[:], in_=total[:])
+            nc.vector.tensor_scalar_mul(p_fac[h][:], p_inv[:], GAIN)
+
+        spare = psum.tile([P, J], F32, name="spare")
+        nc.tensor.matmul_mx(
+            out=spare[:],
+            lhsT=x_codes[TILES - 1][:].bitcast(FP8X4),
+            lhsT_scale=x_plane[TILES - 1][:],
+            rhs=wc_codes[:].bitcast(FP4X4),
+            rhs_scale=wc_plane[:, 0, :],
+            start=True,
+            stop=True,
+        )
 
         u = []
         for h in range(TILES):
@@ -141,27 +153,27 @@ def tile_list_teacher_at_listed_classes_kernel(
             nc.vector.tensor_copy(listed[:], u[h][:].indirect(offsets[:]))
             return listed
 
-        def finish(h, q, q_fac, p_share, res, pieces):
-            width = J // len(pieces)
-            for i, queue in enumerate(pieces):
+        def finish(h, q, q_inv, q_fac, res, pieces):
+            nc.vector.tensor_scalar_mul(q_fac, q_inv, -GAIN)
+            width = J // pieces
+            for i in range(pieces):
                 cols = slice(i * width, (i + 1) * width)
                 nc.vector.scalar_tensor_tensor(
-                    out=res[:, cols], in0=q[:, cols], scalar=q_fac, in1=p_share[:, cols],
+                    out=res[:, cols], in0=q[:, cols], scalar=q_fac, in1=shares[:, h, cols],
                     op0=ALU.mult, op1=ALU.add,
                 )
-                queue.dma_start(out=out[h * P : (h + 1) * P, cols], in_=res[:, cols])
+                nc.sync.dma_start(out=out[h * P : (h + 1) * P, cols], in_=res[:, cols])
 
         listed0 = gather(0)
         shares = keep.tile([P, TILES, J], F32, name="shares", tag="u0")
-        q0, q_part0 = exp_with_sum("q0", listed0[:], -GAIN)
+        q0, q_sum0 = exp_with_sum("q0", listed0[:])
         for h in range(TILES):
             nc.scalar.activation(out=shares[:, h, :], in_=p[h][:], func=ACT.Identity, scale=p_fac[h][:])
         listed1 = gather(1)
-        tail0 = keep.tile([P, J + 1], F32, name="tail0", tag="u1")
-        nc.vector.reciprocal(out=tail0[:, J : J + 1], in_=q_part0[:])
-        q1, q_part1 = exp_with_sum("q1", listed1[:], -GAIN)
-        finish(0, q0, tail0[:, J : J + 1], shares[:, 0, :], tail0, [nc.sync])
-        q_fac1 = column("q_fac1")
-        res1 = keep.tile([P, J], F32, name="res1")
-        nc.vector.reciprocal(out=q_fac1[:], in_=q_part1[:])
-        finish(1, q1, q_fac1[:], shares[:, 1, :], res1, [nc.sync, nc.scalar])
+        tail0 = keep.tile([P, J + 2], F32, name="tail0", tag="u1")
+        nc.vector.reciprocal(out=tail0[:, J : J + 1], in_=q_sum0[:])
+        q1, q_sum1 = exp_with_sum("q1", listed1[:])
+        finish(0, q0, tail0[:, J : J + 1], tail0[:, J + 1 : J + 2], tail0, 1)
+        tail1 = keep.tile([P, J + 2], F32, name="tail1")
+        nc.vector.reciprocal(out=tail1[:, J : J + 1], in_=q_sum1[:])
+        finish(1, q1, tail1[:, J : J + 1], tail1[:, J + 1 : J + 2], tail1, 2)

@@ -19,25 +19,29 @@ AX = mybir.AxisListType
 
 P = 128
 PACK = 4
+QUADRANT = 32
+SCALE_ROWS = 4
+LIST_ROWS = 16
 BANK = 512
-QUADS = 4
+NARROW = 128
 PASSES = L // (P * PACK)
 TILES = T // P
 GAIN = 256.0
 
 
-def scale_plane(nc, pool, name, scales):
-    passes, rows, width = scales.shape
-    tile = pool.tile([P, passes * width + 4], U8, name=name, align_bytes=64)
-    nc.vector.memset(tile[:].bitcast(I32), 0)
-    return tile[:, 0 : passes * width].rearrange("p (z n) -> p z n", z=passes)
+def cleared_plane(nc, pool, name, scales):
+    passes, width = scales.shape[0], scales.shape[2]
+    plane = pool.tile([P, passes, width], U8, name=name, align_bytes=64)
+    nc.vector.memset(plane[:].bitcast(I32), 0)
+    return plane
 
 
 def load_scales(queue, plane, scales):
-    for q in range(QUADS):
+    for q in range(P // QUADRANT):
+        rows = scales[:, SCALE_ROWS * q : SCALE_ROWS * (q + 1), :]
         queue.dma_start(
-            out=plane[32 * q : 32 * q + 4, :, :].bitcast(I32),
-            in_=scales[:, 4 * q : 4 * q + 4, :].rearrange("z r n -> r z n").bitcast(I32),
+            out=plane[QUADRANT * q : QUADRANT * q + SCALE_ROWS, :, :].bitcast(I32),
+            in_=rows.rearrange("z r n -> r z n").bitcast(I32),
         )
 
 
@@ -49,17 +53,17 @@ def tile_list_teacher_at_listed_classes_kernel(
         keep = ctx.enter_context(tc.tile_pool(name="keep", bufs=1))
         psum = ctx.enter_context(tc.psum_pool(name="psum", bufs=1))
 
-        offsets = keep.tile([P, J // 16], U16, name="offsets")
+        offsets = keep.tile([P, J // LIST_ROWS], U16, name="offsets")
         xt_raw = keep.tile([P, PACK, T], F32, name="xt_raw")
         wc_codes = keep.tile([P, 2 * J], U8, name="wc_codes", align_bytes=64)
         xl_codes = keep.tile([P, PASSES, T], U32, name="xl_codes", align_bytes=64)
         wl_codes = keep.tile([P, PASSES, 2 * C], U8, name="wl_codes", align_bytes=64)
-        wc_plane = scale_plane(nc, keep, "wc_plane", wc_scales)
-        wl_plane = scale_plane(nc, keep, "wl_plane", wl_scales)
-        xl_plane = scale_plane(nc, keep, "xl_plane", xl_scales)
+        wc_plane = cleared_plane(nc, keep, "wc_plane", wc_scales)
+        wl_plane = cleared_plane(nc, keep, "wl_plane", wl_scales)
+        xl_plane = cleared_plane(nc, keep, "xl_plane", xl_scales)
 
         nc.sync.dma_start(offsets[:], offs)
-        nc.sync.dma_start(out=xt_raw[:], in_=xt.rearrange("(p j) t -> p j t", j=PACK))
+        nc.sync.dma_start(out=xt_raw[:], in_=xt.rearrange("(p r) t -> p r t", r=PACK))
         nc.sync.dma_start(out=wc_codes[:].bitcast(I32), in_=wc_words[0].bitcast(I32))
         load_scales(nc.scalar, wc_plane, wc_scales)
         nc.gpsimd.dma_start(
@@ -68,7 +72,7 @@ def tile_list_teacher_at_listed_classes_kernel(
         )
         nc.gpsimd.dma_start(
             out=xl_codes[:].bitcast(I32),
-            in_=xl_words.rearrange("z p c r -> p z (c r)").bitcast(I32),
+            in_=xl_words.rearrange("z p t r -> p z (t r)").bitcast(I32),
         )
         load_scales(nc.sync, wl_plane, wl_scales)
         load_scales(nc.sync, xl_plane, xl_scales)
@@ -78,17 +82,19 @@ def tile_list_teacher_at_listed_classes_kernel(
 
         def exp_with_sum(name, logits):
             negmax, total = column(name + "_negmax"), column(name + "_sum")
-            e = keep.tile([P, J], F32, name=name)
+            values = keep.tile([P, J], F32, name=name)
             nc.vector.tensor_reduce(out=negmax[:], in_=logits, axis=AX.X, op=ALU.max, negate=True)
-            nc.scalar.activation(out=e[:], in_=logits, func=ACT.Exp, bias=negmax[:], accum_out=total[:])
-            return e, total
+            nc.scalar.activation(
+                out=values[:], in_=logits, func=ACT.Exp, bias=negmax[:], accum_out=total[:]
+            )
+            return values, total
 
-        grouped, x_codes, x_plane, z = [], [], [], []
+        grouped, x_codes, x_plane = [], [], []
         for h in range(TILES):
             grouped.append(keep.tile([P, P, PACK], BF16, name=f"grouped{h}", align_bytes=64))
             nc.vector.tensor_copy(
                 out=grouped[h][:],
-                in_=xt_raw[:, :, h * P : (h + 1) * P].rearrange("p j t -> p t j"),
+                in_=xt_raw[:, :, h * P : (h + 1) * P].rearrange("p r t -> p t r"),
             )
         for h in range(TILES):
             x_codes.append(keep.tile([P, P], U32, name=f"x_codes{h}", align_bytes=64))
@@ -96,11 +102,11 @@ def tile_list_teacher_at_listed_classes_kernel(
             nc.vector.quantize_mx(
                 out=x_codes[h][:].bitcast(FP8X4),
                 scales=x_plane[h][:],
-                in_=grouped[h][:].rearrange("p t j -> p (t j)"),
+                in_=grouped[h][:].rearrange("p t r -> p (t r)"),
             )
-        p, p_fac = [], []
-        for h in range(TILES):
-            z = psum.tile([P, J], F32, name=f"z{h}")
+
+        def student_sums(h, name):
+            z = psum.tile([P, J], F32, name=name)
             nc.tensor.matmul_mx(
                 out=z[:],
                 lhsT=x_codes[h][:].bitcast(FP8X4),
@@ -110,70 +116,80 @@ def tile_list_teacher_at_listed_classes_kernel(
                 start=True,
                 stop=True,
             )
-            e, total = exp_with_sum(f"p{h}", z[:])
-            p.append(e)
-            p_inv = column(f"p_inv{h}")
-            p_fac.append(column(f"p_fac{h}"))
-            nc.vector.reciprocal(out=p_inv[:], in_=total[:])
-            nc.vector.tensor_scalar_mul(p_fac[h][:], p_inv[:], GAIN)
+            return z
 
-        spare = psum.tile([P, J], F32, name="spare")
-        nc.tensor.matmul_mx(
-            out=spare[:],
-            lhsT=x_codes[TILES - 1][:].bitcast(FP8X4),
-            lhsT_scale=x_plane[TILES - 1][:],
-            rhs=wc_codes[:].bitcast(FP4X4),
-            rhs_scale=wc_plane[:, 0, :],
-            start=True,
-            stop=True,
-        )
-
-        u = []
+        p, p_factor = [], []
         for h in range(TILES):
-            u.append(keep.tile([P, C], F32, name=f"u{h}", tag=f"u{h}"))
-            for b in range(C // BANK):
-                acc = psum.tile([P, BANK], F32, name=f"acc{h}{b}")
+            values, total = exp_with_sum(f"p{h}", student_sums(h, f"z{h}")[:])
+            p.append(values)
+            p_inverse = column(f"p_inverse{h}")
+            p_factor.append(column(f"p_factor{h}"))
+            nc.vector.reciprocal(out=p_inverse[:], in_=total[:])
+            nc.vector.tensor_scalar_mul(p_factor[h][:], p_inverse[:], GAIN)
+
+        student_sums(TILES - 1, "warm_up")
+
+        def teacher_sums(h, first, width, group):
+            acc = psum.tile([P, width], F32, name=f"acc{h}_{first}")
+            for c0 in range(0, width, group):
+                cols = slice(first + c0, first + c0 + group)
                 for g in range(PASSES):
                     nc.tensor.matmul_mx(
-                        out=acc[:],
+                        out=acc[:, c0 : c0 + group],
                         lhsT=xl_codes[:, g, h * P : (h + 1) * P].bitcast(FP8X4),
                         lhsT_scale=xl_plane[:, g, h * P : (h + 1) * P],
-                        rhs=wl_codes[:, g, 2 * b * BANK : 2 * (b + 1) * BANK].bitcast(FP4X4),
-                        rhs_scale=wl_plane[:, g, b * BANK : (b + 1) * BANK],
+                        rhs=wl_codes[:, g, 2 * cols.start : 2 * cols.stop].bitcast(FP4X4),
+                        rhs_scale=wl_plane[:, g, cols],
                         start=(g == 0),
                         stop=(g == PASSES - 1),
                     )
-                if h == 0 and b == 1:
-                    nc.vector.tensor_copy(out=u[h][:, b * BANK : (b + 1) * BANK], in_=acc[:])
-                else:
-                    nc.scalar.copy(out=u[h][:, b * BANK : (b + 1) * BANK], in_=acc[:])
+            return acc
+
+        u = [keep.tile([P, C], F32, name=f"u{h}", tag=f"u{h}") for h in range(TILES)]
+        nc.vector.tensor_copy(out=u[0][:, 0:BANK], in_=teacher_sums(0, 0, BANK, BANK)[:])
+        for first in range(BANK, C, BANK // 2):
+            acc = teacher_sums(0, first, BANK // 2, NARROW)
+            nc.scalar.copy(out=u[0][:, first : first + BANK // 2], in_=acc[:])
+        for first in range(0, C, BANK):
+            acc = teacher_sums(1, first, BANK, BANK)
+            nc.scalar.copy(out=u[1][:, first : first + BANK], in_=acc[:])
 
         def gather(h):
-            listed = keep.tile([P, J], F32, name=f"listed{h}")
+            listed = keep.tile([P, J], F32, name=f"listed{h}", tag=f"listed{h}")
             nc.vector.tensor_copy(listed[:], u[h][:].indirect(offsets[:]))
             return listed
 
-        def finish(h, q, q_inv, q_fac, res, pieces):
-            nc.vector.tensor_scalar_mul(q_fac, q_inv, -GAIN)
+        def finish(h, q, tail, pieces):
+            q_factor = tail[:, J + 1 : J + 2]
+            nc.vector.tensor_scalar_mul(q_factor, tail[:, J : J + 1], -GAIN)
             width = J // pieces
             for i in range(pieces):
                 cols = slice(i * width, (i + 1) * width)
                 nc.vector.scalar_tensor_tensor(
-                    out=res[:, cols], in0=q[:, cols], scalar=q_fac, in1=shares[:, h, cols],
-                    op0=ALU.mult, op1=ALU.add,
+                    out=tail[:, cols],
+                    in0=q[:, cols],
+                    scalar=q_factor,
+                    in1=shares[:, h, cols],
+                    op0=ALU.mult,
+                    op1=ALU.add,
                 )
-                nc.sync.dma_start(out=out[h * P : (h + 1) * P, cols], in_=res[:, cols])
+                nc.sync.dma_start(out=out[h * P : (h + 1) * P, cols], in_=tail[:, cols])
 
         listed0 = gather(0)
-        shares = keep.tile([P, TILES, J], F32, name="shares", tag="u0")
-        q0, q_sum0 = exp_with_sum("q0", listed0[:])
+        q0, q0_sum = exp_with_sum("q0", listed0[:])
+
+        shares = keep.tile([P, TILES, J], F32, name="shares", tag="listed0")
         for h in range(TILES):
-            nc.scalar.activation(out=shares[:, h, :], in_=p[h][:], func=ACT.Identity, scale=p_fac[h][:])
+            nc.scalar.activation(
+                out=shares[:, h, :], in_=p[h][:], func=ACT.Identity, scale=p_factor[h][:]
+            )
+
         listed1 = gather(1)
         tail0 = keep.tile([P, J + 2], F32, name="tail0", tag="u1")
-        nc.vector.reciprocal(out=tail0[:, J : J + 1], in_=q_sum0[:])
-        q1, q_sum1 = exp_with_sum("q1", listed1[:])
-        finish(0, q0, tail0[:, J : J + 1], tail0[:, J + 1 : J + 2], tail0, 1)
+        nc.vector.reciprocal(out=tail0[:, J : J + 1], in_=q0_sum[:])
+        q1, q1_sum = exp_with_sum("q1", listed1[:])
+        finish(0, q0, tail0, pieces=1)
+
         tail1 = keep.tile([P, J + 2], F32, name="tail1")
-        nc.vector.reciprocal(out=tail1[:, J : J + 1], in_=q_sum1[:])
-        finish(1, q1, tail1[:, J : J + 1], tail1[:, J + 1 : J + 2], tail1, 2)
+        nc.vector.reciprocal(out=tail1[:, J : J + 1], in_=q1_sum[:])
+        finish(1, q1, tail1, pieces=2)

from contextlib import ExitStack

import concourse.mybir as mybir

K, L, T, C, J = 512, 1024, 256, 1024, 512
FLOPS = 2 * T * (K * J + L * C)

F32 = mybir.dt.float32
BF16 = mybir.dt.bfloat16
I32 = mybir.dt.int32
U32 = mybir.dt.uint32
U16 = mybir.dt.uint16
U8 = mybir.dt.uint8
FP8X4 = mybir.dt.float8_e4m3fn_x4
FP4X4 = mybir.dt.float4_e2m1fn_x4
ALU = mybir.AluOpType
ACT = mybir.ActivationFunctionType
AX = mybir.AxisListType

P = 128
PACK = 4
QUADRANT = 32
SCALE_ROWS = 4
LIST_ROWS = 16
BANK = 512
NARROW = 128
PASSES = L // (P * PACK)
TILES = T // P
GAIN = 256.0


def cleared_plane(nc, pool, name, scales):
    passes, width = scales.shape[0], scales.shape[2]
    plane = pool.tile([P, passes, width], U8, name=name, align_bytes=64)
    nc.vector.memset(plane[:].bitcast(I32), 0)
    return plane


def load_scales(queue, plane, scales):
    for q in range(P // QUADRANT):
        rows = scales[:, SCALE_ROWS * q : SCALE_ROWS * (q + 1), :]
        queue.dma_start(
            out=plane[QUADRANT * q : QUADRANT * q + SCALE_ROWS, :, :].bitcast(I32),
            in_=rows.rearrange("z r n -> r z n").bitcast(I32),
        )


def tile_list_teacher_at_listed_classes_kernel(
    tc, xt, wc_words, wc_scales, xl_words, xl_scales, wl_words, wl_scales, offs, out
):
    nc = tc.nc
    with ExitStack() as ctx:
        keep = ctx.enter_context(tc.tile_pool(name="keep", bufs=1))
        psum = ctx.enter_context(tc.psum_pool(name="psum", bufs=1))

        offsets = keep.tile([P, J // LIST_ROWS], U16, name="offsets")
        xt_raw = keep.tile([P, PACK, T], F32, name="xt_raw")
        wc_codes = keep.tile([P, 2 * J], U8, name="wc_codes", align_bytes=64)
        xl_codes = keep.tile([P, PASSES, T], U32, name="xl_codes", align_bytes=64)
        wl_codes = keep.tile([P, PASSES, 2 * C], U8, name="wl_codes", align_bytes=64)
        wc_plane = cleared_plane(nc, keep, "wc_plane", wc_scales)
        wl_plane = cleared_plane(nc, keep, "wl_plane", wl_scales)
        xl_plane = cleared_plane(nc, keep, "xl_plane", xl_scales)

        nc.sync.dma_start(offsets[:], offs)
        nc.sync.dma_start(out=xt_raw[:], in_=xt.rearrange("(p r) t -> p r t", r=PACK))
        nc.sync.dma_start(out=wc_codes[:].bitcast(I32), in_=wc_words[0].bitcast(I32))
        load_scales(nc.scalar, wc_plane, wc_scales)
        nc.gpsimd.dma_start(
            out=wl_codes[:].bitcast(I32),
            in_=wl_words.rearrange("z p b -> p z b").bitcast(I32),
        )
        nc.gpsimd.dma_start(
            out=xl_codes[:].bitcast(I32),
            in_=xl_words.rearrange("z p t r -> p z (t r)").bitcast(I32),
        )
        load_scales(nc.sync, wl_plane, wl_scales)
        load_scales(nc.sync, xl_plane, xl_scales)

        def column(name):
            return keep.tile([P, 1], F32, name=name)

        def exp_with_sum(name, logits):
            negmax, total = column(name + "_negmax"), column(name + "_sum")
            values = keep.tile([P, J], F32, name=name)
            nc.vector.tensor_reduce(out=negmax[:], in_=logits, axis=AX.X, op=ALU.max, negate=True)
            nc.scalar.activation(
                out=values[:], in_=logits, func=ACT.Exp, bias=negmax[:], accum_out=total[:]
            )
            return values, total

        grouped, x_codes, x_plane = [], [], []
        for h in range(TILES):
            grouped.append(keep.tile([P, P, PACK], BF16, name=f"grouped{h}", align_bytes=64))
            nc.vector.tensor_copy(
                out=grouped[h][:],
                in_=xt_raw[:, :, h * P : (h + 1) * P].rearrange("p r t -> p t r"),
            )
        for h in range(TILES):
            x_codes.append(keep.tile([P, P], U32, name=f"x_codes{h}", align_bytes=64))
            x_plane.append(keep.tile([P, P], U8, name=f"x_plane{h}", align_bytes=64))
            nc.vector.quantize_mx(
                out=x_codes[h][:].bitcast(FP8X4),
                scales=x_plane[h][:],
                in_=grouped[h][:].rearrange("p t r -> p (t r)"),
            )

        def student_sums(h, name):
            z = psum.tile([P, J], F32, name=name)
            nc.tensor.matmul_mx(
                out=z[:],
                lhsT=x_codes[h][:].bitcast(FP8X4),
                lhsT_scale=x_plane[h][:],
                rhs=wc_codes[:].bitcast(FP4X4),
                rhs_scale=wc_plane[:, 0, :],
                start=True,
                stop=True,
            )
            return z

        p, p_factor = [], []
        for h in range(TILES):
            values, total = exp_with_sum(f"p{h}", student_sums(h, f"z{h}")[:])
            p.append(values)
            p_inverse = column(f"p_inverse{h}")
            p_factor.append(column(f"p_factor{h}"))
            nc.vector.reciprocal(out=p_inverse[:], in_=total[:])
            nc.vector.tensor_scalar_mul(p_factor[h][:], p_inverse[:], GAIN)

        student_sums(TILES - 1, "warm_up")

        def teacher_sums(h, first, width, group):
            acc = psum.tile([P, width], F32, name=f"acc{h}_{first}")
            for c0 in range(0, width, group):
                cols = slice(first + c0, first + c0 + group)
                for g in range(PASSES):
                    nc.tensor.matmul_mx(
                        out=acc[:, c0 : c0 + group],
                        lhsT=xl_codes[:, g, h * P : (h + 1) * P].bitcast(FP8X4),
                        lhsT_scale=xl_plane[:, g, h * P : (h + 1) * P],
                        rhs=wl_codes[:, g, 2 * cols.start : 2 * cols.stop].bitcast(FP4X4),
                        rhs_scale=wl_plane[:, g, cols],
                        start=(g == 0),
                        stop=(g == PASSES - 1),
                    )
            return acc

        u = [keep.tile([P, C], F32, name=f"u{h}", tag=f"u{h}") for h in range(TILES)]
        nc.vector.tensor_copy(out=u[0][:, 0:BANK], in_=teacher_sums(0, 0, BANK, BANK)[:])
        for first in range(BANK, C, BANK // 2):
            acc = teacher_sums(0, first, BANK // 2, NARROW)
            nc.scalar.copy(out=u[0][:, first : first + BANK // 2], in_=acc[:])
        for first in range(0, C, BANK):
            acc = teacher_sums(1, first, BANK, BANK)
            nc.scalar.copy(out=u[1][:, first : first + BANK], in_=acc[:])

        def gather(h):
            listed = keep.tile([P, J], F32, name=f"listed{h}", tag=f"listed{h}")
            nc.vector.tensor_copy(listed[:], u[h][:].indirect(offsets[:]))
            return listed

        def finish(h, q, tail, pieces):
            q_factor = tail[:, J + 1 : J + 2]
            nc.vector.tensor_scalar_mul(q_factor, tail[:, J : J + 1], -GAIN)
            width = J // pieces
            for i in range(pieces):
                cols = slice(i * width, (i + 1) * width)
                nc.vector.scalar_tensor_tensor(
                    out=tail[:, cols],
                    in0=q[:, cols],
                    scalar=q_factor,
                    in1=shares[:, h, cols],
                    op0=ALU.mult,
                    op1=ALU.add,
                )
                nc.sync.dma_start(out=out[h * P : (h + 1) * P, cols], in_=tail[:, cols])

        listed0 = gather(0)
        q0, q0_sum = exp_with_sum("q0", listed0[:])

        shares = keep.tile([P, TILES, J], F32, name="shares", tag="listed0")
        for h in range(TILES):
            nc.scalar.activation(
                out=shares[:, h, :], in_=p[h][:], func=ACT.Identity, scale=p_factor[h][:]
            )

        listed1 = gather(1)
        tail0 = keep.tile([P, J + 2], F32, name="tail0", tag="u1")
        nc.vector.reciprocal(out=tail0[:, J : J + 1], in_=q0_sum[:])
        q1, q1_sum = exp_with_sum("q1", listed1[:])
        finish(0, q0, tail0, pieces=1)

        tail1 = keep.tile([P, J + 2], F32, name="tail1")
        nc.vector.reciprocal(out=tail1[:, J : J + 1], in_=q1_sum[:])
        finish(1, q1, tail1, pieces=2)
